import numpy as np
import ml_dtypes

BF16 = ml_dtypes.bfloat16


def bf(x):
    return np.asarray(x, np.float32).astype(BF16)


def f32(x):
    return np.asarray(x, np.float32)


def f64(x):
    return np.asarray(x).astype(np.float64)


def striped(idx):
    return np.tile(idx.reshape(-1, 16).T, (8, 1))


def rows(idx, k):
    return np.tile(idx, (k, 1))


def look(tab, idx):
    return np.take_along_axis(f64(tab), rows(idx, len(tab)), axis=1)


K, S, V, N, M = 512, 2048, 1024, 1024, 128


def setup_inputs():
    return {"tab": f32(np.random.standard_normal((K, S))), "qry": f32(np.random.standard_normal((K, V))), "w": bf(np.random.uniform(0.0, 2.0, (K, M)) / K), "offs": striped(np.random.randint(0, S, N))}


def reference(tab, qry, w, offs):
    idx = offs[:16].T.reshape(-1)
    x = np.abs(look(tab, idx) - f64(qry))
    y = f64(w).T @ x
    return y

@@ -1,0 +1,60 @@
+import concourse.mybir as mybir
+
+F32, BF16, U16 = mybir.dt.float32, mybir.dt.bfloat16, mybir.dt.uint16
+SUBTRACT = mybir.AluOpType.subtract
+ABS = mybir.ActivationFunctionType.Abs
+
+P = 128
+BANK = 512
+
+FLOPS = 2 * 512 * 128 * 1024
+
+
+def tile_lookup_manh_sub_none_kernel(tc, tab, qry, w, offs, out):
+    nc = tc.nc
+    rows, columns = tab.shape
+    count = qry.shape[1]
+    metrics = w.shape[1]
+    blocks = rows // P
+
+    tab_rows = tab.rearrange("(p b) s -> p b s", b=blocks)
+    qry_rows = qry.rearrange("(p b) j -> p b j", b=blocks)
+    w_rows = w.rearrange("(p b) m -> p (b m)", b=blocks)
+
+    with (
+        tc.tile_pool(name="held", bufs=1) as held,
+        tc.tile_pool(name="loads", bufs=blocks) as loads,
+        tc.tile_pool(name="work", bufs=2) as work,
+        tc.psum_pool(name="psum", bufs=1) as psum,
+    ):
+        offsets = held.tile([P, count // 16], U16, name="offsets")
+        nc.sync.dma_start(offsets[:], offs)
+        weights = held.tile([P, blocks * metrics], BF16, name="weights")
+        nc.scalar.dma_start(weights[:], w_rows)
+
+        sums = [psum.tile([P, BANK], F32, name=f"sums{h}") for h in range(count // BANK)]
+
+        for b in range(blocks):
+            table = loads.tile([P, columns], F32, name="table")
+            nc.sync.dma_start(table[:], tab_rows[:, b, :])
+            query = loads.tile([P, count], F32, name="query")
+            nc.sync.dma_start(query[:], qry_rows[:, b, :])
+
+            difference = work.tile([P, count], F32, name="difference")
+            nc.vector.tensor_tensor(difference[:], table[:].indirect(offsets[:]), query[:], SUBTRACT)
+            distance = work.tile([P, count], BF16, name="distance")
+            nc.scalar.activation(distance[:], difference[:], ABS)
+
+            for h in range(count // BANK):
+                nc.tensor.matmul(
+                    sums[h][:],
+                    weights[:, b * metrics : (b + 1) * metrics],
+                    distance[:, h * BANK : (h + 1) * BANK],
+                    start=(b == 0),
+                    stop=(b == blocks - 1),
+                )
+
+        for h in range(count // BANK):
+            result = held.tile([P, BANK], F32, name=f"result{h}")
+            nc.vector.tensor_copy(result[:], sums[h][:])
+            nc.sync.dma_start(out[:, h * BANK : (h + 1) * BANK], result[:])

@@ -5,7 +5,8 @@ SUBTRACT = mybir.AluOpType.subtract
 ABS = mybir.ActivationFunctionType.Abs
 
 P = 128
-BANK = 512
+PIECE = 256
+QUERY_PIECE = 512
 
 FLOPS = 2 * 512 * 128 * 1024
 
@@ -32,29 +33,36 @@ def tile_lookup_manh_sub_none_kernel(tc, tab, qry, w, offs, out):
         weights = held.tile([P, blocks * metrics], BF16, name="weights")
         nc.scalar.dma_start(weights[:], w_rows)
 
-        sums = [psum.tile([P, BANK], F32, name=f"sums{h}") for h in range(count // BANK)]
+        sums = [psum.tile([P, PIECE], F32, name=f"sums{j}") for j in range(0, count, PIECE)]
 
         for b in range(blocks):
+            last = b == blocks - 1
             table = loads.tile([P, columns], F32, name="table")
             nc.sync.dma_start(table[:], tab_rows[:, b, :])
             query = loads.tile([P, count], F32, name="query")
-            nc.sync.dma_start(query[:], qry_rows[:, b, :])
+            load_width = QUERY_PIECE if last else count
+            for j in range(0, count, load_width):
+                nc.sync.dma_start(query[:, j : j + load_width], qry_rows[:, b, j : j + load_width])
 
+            gather_width = PIECE if last else count
             difference = work.tile([P, count], F32, name="difference")
-            nc.vector.tensor_tensor(difference[:], table[:].indirect(offsets[:]), query[:], SUBTRACT)
             distance = work.tile([P, count], BF16, name="distance")
-            nc.scalar.activation(distance[:], difference[:], ABS)
+            for j in range(0, count, gather_width):
+                piece = slice(j, j + gather_width)
+                picked = table[:].indirect(offsets[:, j // 16 : (j + gather_width) // 16])
+                nc.vector.tensor_tensor(difference[:, piece], picked, query[:, piece], SUBTRACT)
+                nc.scalar.activation(distance[:, piece], difference[:, piece], ABS)
 
-            for h in range(count // BANK):
+            for k in range(count // PIECE):
                 nc.tensor.matmul(
-                    sums[h][:],
+                    sums[k][:],
                     weights[:, b * metrics : (b + 1) * metrics],
-                    distance[:, h * BANK : (h + 1) * BANK],
+                    distance[:, k * PIECE : (k + 1) * PIECE],
                     start=(b == 0),
-                    stop=(b == blocks - 1),
+                    stop=last,
                 )
 
-        for h in range(count // BANK):
-            result = held.tile([P, BANK], F32, name=f"result{h}")
-            nc.vector.tensor_copy(result[:], sums[h][:])
-            nc.sync.dma_start(out[:, h * BANK : (h + 1) * BANK], result[:])
+        for k in range(count // PIECE):
+            result = held.tile([P, PIECE], F32, name=f"result{k}")
+            nc.scalar.copy(result[:], sums[k][:])
+            nc.sync.dma_start(out[:, k * PIECE : (k + 1) * PIECE], result[:])

import concourse.mybir as mybir

F32, BF16, U16 = mybir.dt.float32, mybir.dt.bfloat16, mybir.dt.uint16
SUBTRACT = mybir.AluOpType.subtract
ABS = mybir.ActivationFunctionType.Abs

P = 128
PIECE = 256
QUERY_PIECE = 512

FLOPS = 2 * 512 * 128 * 1024


def tile_lookup_manh_sub_none_kernel(tc, tab, qry, w, offs, out):
    nc = tc.nc
    rows, columns = tab.shape
    count = qry.shape[1]
    metrics = w.shape[1]
    blocks = rows // P

    tab_rows = tab.rearrange("(p b) s -> p b s", b=blocks)
    qry_rows = qry.rearrange("(p b) j -> p b j", b=blocks)
    w_rows = w.rearrange("(p b) m -> p (b m)", b=blocks)

    with (
        tc.tile_pool(name="held", bufs=1) as held,
        tc.tile_pool(name="loads", bufs=blocks) as loads,
        tc.tile_pool(name="work", bufs=2) as work,
        tc.psum_pool(name="psum", bufs=1) as psum,
    ):
        offsets = held.tile([P, count // 16], U16, name="offsets")
        nc.sync.dma_start(offsets[:], offs)
        weights = held.tile([P, blocks * metrics], BF16, name="weights")
        nc.scalar.dma_start(weights[:], w_rows)

        sums = [psum.tile([P, PIECE], F32, name=f"sums{j}") for j in range(0, count, PIECE)]

        for b in range(blocks):
            last = b == blocks - 1
            table = loads.tile([P, columns], F32, name="table")
            nc.sync.dma_start(table[:], tab_rows[:, b, :])
            query = loads.tile([P, count], F32, name="query")
            load_width = QUERY_PIECE if last else count
            for j in range(0, count, load_width):
                nc.sync.dma_start(query[:, j : j + load_width], qry_rows[:, b, j : j + load_width])

            gather_width = PIECE if last else count
            difference = work.tile([P, count], F32, name="difference")
            distance = work.tile([P, count], BF16, name="distance")
            for j in range(0, count, gather_width):
                piece = slice(j, j + gather_width)
                picked = table[:].indirect(offsets[:, j // 16 : (j + gather_width) // 16])
                nc.vector.tensor_tensor(difference[:, piece], picked, query[:, piece], SUBTRACT)
                nc.scalar.activation(distance[:, piece], difference[:, piece], ABS)

            for k in range(count // PIECE):
                nc.tensor.matmul(
                    sums[k][:],
                    weights[:, b * metrics : (b + 1) * metrics],
                    distance[:, k * PIECE : (k + 1) * PIECE],
                    start=(b == 0),
                    stop=last,
                )

        for k in range(count // PIECE):
            result = held.tile([P, PIECE], F32, name=f"result{k}")
            nc.scalar.copy(result[:], sums[k][:])
            nc.sync.dma_start(out[:, k * PIECE : (k + 1) * PIECE], result[:])
